import numpy as np
import ml_dtypes


def mxq(x, axis, fmt="e4m3"):
    dtype, down = {"e4m3": (ml_dtypes.float8_e4m3fn, 7), "e5m2": (ml_dtypes.float8_e5m2, 14)}[fmt]
    v = np.moveaxis(np.asarray(x, np.float32).astype(ml_dtypes.bfloat16).astype(np.float64), axis, -1)
    blocks = v.reshape(v.shape[:-1] + (-1, 32))
    amax = np.abs(blocks).max(-1, keepdims=True)
    byte = np.maximum(np.where(amax > 0, np.frexp(amax)[1] - 1 + 127, 0) - down, 1)
    scale = np.exp2(byte - 127.0)
    codes = (blocks / scale).astype(np.float32).astype(dtype).astype(np.float64)
    return np.moveaxis((codes * scale).reshape(v.shape), -1, axis)


WIDE = False


def mx_kscale(k):
    if not WIDE:
        return np.ones(k)
    levels = np.array([10, -10, 5, -5, 0])
    if k % 512:
        return np.exp2(np.random.permutation(np.resize(levels, k // 32))).repeat(32)
    a = np.empty((k // 512, 16))
    for p in range(k // 512):
        a[p, :8] = np.random.permutation(np.resize(levels, 8))
        for g in range(8):
            far = levels[np.abs(levels - a[p, g]) >= 10]
            a[p, g + 8] = far[np.random.randint(len(far))]
    return np.exp2(a.ravel()).repeat(32)


def f64(x):
    return np.asarray(x).astype(np.float64)


def striped(idx):
    return np.tile(idx.reshape(-1, 16).T, (8, 1)).astype(np.uint16)


def unstriped(offs):
    return offs[:16].T.reshape(-1).astype(np.int64)


E2M1 = np.array([0.0, 0.5, 1.0, 1.5, 2.0, 3.0, 4.0, 6.0, -0.0, -0.5, -1.0, -1.5, -2.0, -3.0, -4.0, -6.0])


def pack_weight(w, fmt):
    k, n = w.shape
    w = f64(np.asarray(w, np.float32).astype(ml_dtypes.bfloat16)).reshape(k // 32, 32, n)
    amax = np.abs(w).max(1)
    if fmt == "e4m3":
        byte = np.frexp(amax)[1] - 1 + 127 - 7
    else:
        mant, ex = np.frexp(amax / 6.0)
        byte = np.where(mant > 0.5, ex, ex - 1) + 127
    byte = np.clip(np.where(amax > 0, byte, 1), 1, 254)
    scaled = (w * np.exp2(127.0 - byte)[:, None, :]).reshape(k, n).astype(np.float32)
    by_word = np.ascontiguousarray(scaled.reshape(k // 512, 128, 4, n).transpose(0, 1, 3, 2))
    if fmt == "e4m3":
        words = by_word.astype(ml_dtypes.float8_e4m3fn).view(np.uint8)
    else:
        c = by_word.astype(ml_dtypes.float4_e2m1fn).view(np.uint8) & 0xF
        words = (c[..., 0::2] | (c[..., 1::2] << 4)).reshape(k // 512, 128, 2 * n)
    return np.ascontiguousarray(words), np.ascontiguousarray(byte.astype(np.uint8).reshape(k // 512, 16, n))


def unpack_weight(words, scales, fmt):
    g, _, n = scales.shape
    words = np.ascontiguousarray(words).reshape(g, 128, n, -1)
    if fmt == "e4m3":
        vals = words.view(ml_dtypes.float8_e4m3fn).astype(np.float64)
    else:
        nib = np.empty((g, 128, n, 4), np.uint8)
        nib[..., 0::2] = words & 0xF
        nib[..., 1::2] = words >> 4
        vals = E2M1[nib]
    vals = vals * np.repeat(np.exp2(scales.astype(np.float64) - 127.0), 8, axis=1)[..., None]
    return vals.transpose(0, 1, 3, 2).reshape(g * 512, n)


K, T, E, N = 1024, 768, 6, 256
COUNTS = (128, 128, 128, 384, 512, 256)
STARTS = np.cumsum((0,) + COUNTS)
K8 = 512


def by_expert(wq, xq):
    return np.concatenate([wq[e].T @ xq[:, STARTS[e]:STARTS[e + 1]] for e in range(E)], axis=1)


def setup_inputs():
    n = np.random.standard_normal
    s = mx_kscale(K)[:, None]
    both = np.repeat(np.arange(E), COUNTS)
    pair = np.stack([both[:T], both[T:]])[:, np.random.permutation(T)]
    pair = np.where(np.random.rand(T) < 0.5, pair, pair[::-1])
    for _ in range(8):
        s_, t_ = np.random.permutation(T).reshape(2, -1); r = np.random.randint(2, size=T // 2); q = np.random.randint(2, size=T // 2); x, y = pair[r, s_].copy(), pair[q, t_].copy()
        ok = (pair[1 - r, s_] != y) & (pair[1 - q, t_] != x); pair[r[ok], s_[ok]] = y[ok]; pair[q[ok], t_[ok]] = x[ok]
    order = np.argsort(pair.reshape(-1), kind="stable")
    slot_token = order % T; pos = np.empty(2 * T, np.int64); pos[order] = np.arange(2 * T); pos = pos.reshape(2, T)
    g = np.random.uniform(0.2, 0.8, T)
    w = n((E, K, N)) / np.sqrt(K) / s[None]
    w8 = [pack_weight(m[:K8], "e4m3") for m in w]
    w4 = [pack_weight(m[K8:], "e2m1") for m in w]
    return {
        "xT": (n((K, T)) * s).astype(np.float32),
        "w8_words": np.stack([m[0] for m in w8]),
        "w8_scales": np.stack([m[1] for m in w8]),
        "w4_words": np.stack([m[0] for m in w4]),
        "w4_scales": np.stack([m[1] for m in w4]),
        "gate": np.stack([np.tile(g, (N, 1)), np.tile(1.0 - g, (N, 1))]).astype(np.float32),
        "offs": striped(slot_token),
        "pos1": striped(pos[0]),
        "pos2": striped(pos[1]),
    }


def reference(xT, w8_words, w8_scales, w4_words, w4_scales, gate, offs, pos1, pos2):
    idx = unstriped(offs)
    w = np.stack([np.concatenate([unpack_weight(w8_words[e], w8_scales[e], "e4m3"), unpack_weight(w4_words[e], w4_scales[e], "e2m1")]) for e in range(E)])
    xq = mxq(f64(xT)[:, idx], 0, "e4m3")
    y = by_expert(w, xq)
    return f64(gate[0]) * y[:, unstriped(pos1)] + f64(gate[1]) * y[:, unstriped(pos2)]

@@ -1,0 +1,178 @@
+from contextlib import ExitStack
+
+import concourse.mybir as mybir
+
+F32 = mybir.dt.float32
+BF16 = mybir.dt.bfloat16
+I32 = mybir.dt.int32
+U32 = mybir.dt.uint32
+U16 = mybir.dt.uint16
+U8 = mybir.dt.uint8
+E4M3X4 = mybir.dt.float8_e4m3fn_x4
+E2M1X4 = mybir.dt.float4_e2m1fn_x4
+MULT = mybir.AluOpType.mult
+ADD = mybir.AluOpType.add
+
+K, T, E, N = 1024, 768, 6, 256
+S = 2 * T
+P = 128
+FLOPS = 2 * K * N * S
+
+STARTS = (0, 128, 256, 384, 768, 1280, 1536)
+CHUNKS = (((0, 256), 256), ((256, 512), 176), ((512, 768), 168))
+CHUNKS1 = (((0, 256), 0), ((256, 512), 0), ((512, 768), 128))
+PIECES0 = ((0, 512), (512, 1024), (1024, 1536))
+GROUPS = (
+    (((768, 1280),), ((768, 1280),), ((4, 0),), ((768, 0, 512),)),
+    (((1280, 1536), (0, 256)), ((1280, 1536), (0, 256)), ((5, 0), (0, 256), (1, 384)), ((1280, 0, 256), (0, 256, 256))),
+    (((256, 768),), ((384, 768),), ((3, 0),), ((384, 0, 384),)),
+    ((), ((256, 384),), ((2, 0),), ((256, 0, 128),)),
+)
+
+
+def tile_moe_rag_lin_none_kernel(
+    tc, xT, w8_words, w8_scales, w4_words, w4_scales, gate, offs, pos1, pos2, out
+):
+    nc = tc.nc
+    with ExitStack() as ctx:
+        keep = ctx.enter_context(tc.tile_pool(name="keep", bufs=1))
+        psum = ctx.enter_context(tc.psum_pool(name="psum", bufs=1))
+
+        offs_t = keep.tile([P, S // 16], U16, name="offs_t")
+        pos_t = [keep.tile([P, T // 16], U16, name=f"pos_t{i}") for i in range(2)]
+        raw = [keep.tile([P, 4, T], F32, name=f"raw{a}") for a in range(2)]
+        words = [keep.tile([P, T], U32, name=f"words{a}", align_bytes=256) for a in range(2)]
+        scales = keep.tile([P, T], U8, name="scales", align_bytes=256)
+        slot_words = [keep.tile([P, S], U32, name=f"slot_words{a}", align_bytes=256) for a in range(2)]
+        slot_scales = keep.tile([P, S], U8, name="slot_scales", align_bytes=256)
+        w8 = keep.tile([P, E * N], U32, name="w8", align_bytes=256)
+        w4 = keep.tile([P, E * 2 * N], U8, name="w4", align_bytes=256)
+        w_scales_i = keep.tile([P, E * N // 4], I32, name="w_scales_i", align_bytes=256)
+        w_scales = w_scales_i[:].bitcast(U8)
+        gates = [[keep.tile([P, T], F32, name=f"gate{c}{h}") for h in range(2)] for c in range(2)]
+        y = [keep.tile([P, S], F32, name=f"y{h}") for h in range(2)]
+        prod = [[keep.tile([P, T], F32, name=f"prod{c}{h}") for h in range(2)] for c in range(2)]
+        res = [keep.tile([P, T], F32, name=f"res{h}") for h in range(2)]
+
+        nc.gpsimd.memset(scales[:], 0)
+        nc.vector.memset(w_scales_i[:], 0)
+
+        def load_x(a, t0, t1):
+            nc.sync.dma_start(
+                out=raw[a][:, :, t0:t1],
+                in_=xT[512 * a : 512 * (a + 1), t0:t1].rearrange("(p j) t -> p j t", j=4),
+            )
+
+        for (t0, t1), v in CHUNKS:
+            load_x(0, t0, t1)
+        nc.sync.dma_start(offs_t[:], offs)
+        for (t0, t1), v in CHUNKS1:
+            load_x(1, t0, t1)
+        for src, row in ((w4_scales, 0), (w8_scales, 4)):
+            for q in range(4):
+                nc.sync.dma_start(
+                    out=w_scales_i[32 * q + row : 32 * q + row + 4, :].rearrange("p (e n) -> p e n", e=E),
+                    in_=src[:, 0, 4 * q : 4 * q + 4, :].rearrange("e q n -> q e n").bitcast(I32),
+                )
+        nc.sync.dma_start(
+            out=w8[:].bitcast(I32).rearrange("p (e n) -> p e n", e=E),
+            in_=w8_words.rearrange("e a p n t -> p (e a) (n t)").bitcast(I32),
+        )
+        nc.sync.dma_start(
+            out=w4[:].bitcast(I32).rearrange("p (e n) -> p e n", e=E),
+            in_=w4_words.rearrange("e a p b -> p (e a) b").bitcast(I32),
+        )
+        nc.sync.dma_start(pos_t[0][:], pos1)
+        nc.sync.dma_start(pos_t[1][:], pos2)
+        for h in range(2):
+            for c in range(2):
+                nc.sync.dma_start(gates[c][h][:], gate[c, P * h : P * (h + 1), :])
+
+        def quantise(a, t0, t1, v):
+            grouped = keep.tile([P, t1 - t0, 4], BF16, name=f"grouped{a}_{t0}", align_bytes=256)
+            if v > 0:
+                nc.vector.tensor_copy(out=grouped[:, :v, :], in_=raw[a][:, :, t0 : t0 + v].rearrange("p j t -> p t j"))
+            if v < t1 - t0:
+                nc.scalar.copy(out=grouped[:, v:, :], in_=raw[a][:, :, t0 + v : t1].rearrange("p j t -> p t j"))
+            return grouped
+
+        def quant(a, t0, t1, grouped):
+            row = 4 * (1 - a)
+            nc.vector.quantize_mx(
+                out=words[a][:, t0:t1].bitcast(E4M3X4),
+                scales=scales[row:P, t0:t1],
+                in_=grouped[:].rearrange("p t j -> p (t j)"),
+            )
+
+        for (t0, t1), v in CHUNKS:
+            quant(0, t0, t1, quantise(0, t0, t1, v))
+
+        def gather(dst, src, s0, s1):
+            nc.vector.tensor_copy(dst[:, s0:s1], src[:].indirect(offs_t[:, s0 // 16 : s1 // 16]))
+
+        g1 = [(t0, t1, quantise(1, t0, t1, 0)) for (t0, t1), v in CHUNKS1[:-1]]
+        for s0, s1 in PIECES0[:2]:
+            gather(slot_words[0], words[0], s0, s1)
+        for t0, t1, g in g1[:1]:
+            quant(1, t0, t1, g)
+        for s0, s1 in PIECES0[2:]:
+            gather(slot_words[0], words[0], s0, s1)
+        for t0, t1, g in g1[1:]:
+            quant(1, t0, t1, g)
+        for (t0, t1), v in CHUNKS1[-1:]:
+            quant(1, t0, t1, quantise(1, t0, t1, v))
+
+        def matmuls(bank, h, expert, col, count):
+            n0 = expert * N + h * P
+            s0 = STARTS[expert]
+            step = 512 if count == 512 else 128
+            for c in range(0, count, step):
+                s = slice(s0 + c, s0 + c + step)
+                nc.tensor.matmul_mx(
+                    out=bank[:, col + c : col + c + step],
+                    lhsT=w4[:, 2 * n0 : 2 * (n0 + P)].bitcast(E2M1X4),
+                    lhsT_scale=w_scales[:, n0 : n0 + P],
+                    rhs=slot_words[1][:, s].bitcast(E4M3X4),
+                    rhs_scale=slot_scales[:, s],
+                    start=True,
+                    stop=False,
+                )
+                nc.tensor.matmul_mx(
+                    out=bank[:, col + c : col + c + step],
+                    lhsT=w8[:, n0 : n0 + P].bitcast(E4M3X4),
+                    lhsT_scale=w_scales[4:P, n0 : n0 + P],
+                    rhs=slot_words[0][:, s].bitcast(E4M3X4),
+                    rhs_scale=slot_scales[4:P, s],
+                    start=False,
+                    stop=True,
+                )
+
+        for b, (byte_pieces, pieces, members, copies) in enumerate(GROUPS):
+            for s0, s1 in byte_pieces:
+                gather(slot_scales, scales, s0, s1)
+            for s0, s1 in pieces:
+                gather(slot_words[1], words[1], s0, s1)
+            for h in range(2):
+                bank = psum.tile([P, 512], F32, name=f"bank{b}{h}")
+                for e, col in members:
+                    matmuls(bank, h, e, col, STARTS[e + 1] - STARTS[e])
+                for s0, col, n in copies:
+                    nc.scalar.copy(out=y[h][:, s0 : s0 + n], in_=bank[:, col : col + n])
+
+        def fetch(c, h, t0, t1):
+            nc.vector.tensor_tensor(
+                prod[c][h][:, t0:t1], y[h][:].indirect(pos_t[c][:, t0 // 16 : t1 // 16]), gates[c][h][:, t0:t1], MULT
+            )
+
+        def total(h, t0, t1):
+            nc.vector.tensor_tensor(res[h][:, t0:t1], prod[0][h][:, t0:t1], prod[1][h][:, t0:t1], ADD)
+            nc.sync.dma_start(out[P * h : P * (h + 1), t0:t1], res[h][:, t0:t1])
+
+        fetch(0, 0, 0, T)
+        fetch(1, 0, 0, T)
+        fetch(0, 1, 0, T)
+        total(0, 0, T)
+        fetch(1, 1, 0, 512)
+        fetch(1, 1, 512, T)
+        total(1, 0, 512)
+        total(1, 512, T)

@@ -19,15 +19,28 @@ P = 128
 FLOPS = 2 * K * N * S
 
 STARTS = (0, 128, 256, 384, 768, 1280, 1536)
-CHUNKS = (((0, 256), 256), ((256, 512), 176), ((512, 768), 168))
-CHUNKS1 = (((0, 256), 0), ((256, 512), 0), ((512, 768), 128))
-PIECES0 = ((0, 512), (512, 1024), (1024, 1536))
-GROUPS = (
-    (((768, 1280),), ((768, 1280),), ((4, 0),), ((768, 0, 512),)),
-    (((1280, 1536), (0, 256)), ((1280, 1536), (0, 256)), ((5, 0), (0, 256), (1, 384)), ((1280, 0, 256), (0, 256, 256))),
-    (((256, 768),), ((384, 768),), ((3, 0),), ((384, 0, 384),)),
-    ((), ((256, 384),), ((2, 0),), ((256, 0, 128),)),
+CHUNKS0 = ((0, 256, 256), (256, 512, 176), (512, 768, 192))
+CHUNKS1 = ((0, 512, (0, 256)), (512, 768, (512,)))
+PIECES0 = ((0, 512), (512, 1024), (1024, 1408), (1408, 1536))
+STEPS = (
+    ("bytes", 960, 1536),
+    ("words", 1280, 1536),
+    ("bytes", 384, 960),
+    ("words", 768, 1280),
+    ("words", 384, 768),
+    ("bytes", 0, 256),
+    ("words", 0, 256),
+    ("bytes", 256, 384),
+    ("words", 256, 384),
 )
+BANKS = (
+    (((5, 0),), ((1280, 0, 256),)),
+    (((4, 0),), ((768, 0, 512),)),
+    (((3, 0),), ((384, 0, 384),)),
+    (((0, 256), (1, 384)), ((0, 256, 256),)),
+    (((2, 0),), ((256, 0, 128),)),
+)
+BANK_OF = (0, 1, 2, 0, 3)
 
 
 def tile_moe_rag_lin_none_kernel(
@@ -63,38 +76,45 @@ def tile_moe_rag_lin_none_kernel(
                 in_=xT[512 * a : 512 * (a + 1), t0:t1].rearrange("(p j) t -> p j t", j=4),
             )
 
-        for (t0, t1), v in CHUNKS:
+        for t0, t1, v in CHUNKS0:
             load_x(0, t0, t1)
         nc.sync.dma_start(offs_t[:], offs)
-        for (t0, t1), v in CHUNKS1:
-            load_x(1, t0, t1)
-        for src, row in ((w4_scales, 0), (w8_scales, 4)):
-            for q in range(4):
-                nc.sync.dma_start(
-                    out=w_scales_i[32 * q + row : 32 * q + row + 4, :].rearrange("p (e n) -> p e n", e=E),
-                    in_=src[:, 0, 4 * q : 4 * q + 4, :].rearrange("e q n -> q e n").bitcast(I32),
-                )
-        nc.sync.dma_start(
-            out=w8[:].bitcast(I32).rearrange("p (e n) -> p e n", e=E),
-            in_=w8_words.rearrange("e a p n t -> p (e a) (n t)").bitcast(I32),
-        )
+        for t0, t1, loads in CHUNKS1:
+            for c0 in loads:
+                load_x(1, c0, c0 + 256)
+        def load_scales(src, row, q):
+            nc.sync.dma_start(
+                out=w_scales_i[32 * q + row : 32 * q + row + 4, :].rearrange("p (e n) -> p e n", e=E),
+                in_=src[:, 0, 4 * q : 4 * q + 4, :].rearrange("e q n -> q e n").bitcast(I32),
+            )
+
+        scale_loads = [(src, row, q) for src, row in ((w4_scales, 0), (w8_scales, 4)) for q in range(4)]
+        for src, row, q in scale_loads[:5]:
+            load_scales(src, row, q)
         nc.sync.dma_start(
             out=w4[:].bitcast(I32).rearrange("p (e n) -> p e n", e=E),
             in_=w4_words.rearrange("e a p b -> p (e a) b").bitcast(I32),
         )
+        nc.sync.dma_start(
+            out=w8[:].bitcast(I32).rearrange("p (e n) -> p e n", e=E),
+            in_=w8_words.rearrange("e a p n t -> p (e a) (n t)").bitcast(I32),
+        )
+        for src, row, q in scale_loads[5:]:
+            load_scales(src, row, q)
         nc.sync.dma_start(pos_t[0][:], pos1)
         nc.sync.dma_start(pos_t[1][:], pos2)
         for h in range(2):
             for c in range(2):
                 nc.sync.dma_start(gates[c][h][:], gate[c, P * h : P * (h + 1), :])
 
-        def quantise(a, t0, t1, v):
-            grouped = keep.tile([P, t1 - t0, 4], BF16, name=f"grouped{a}_{t0}", align_bytes=256)
-            if v > 0:
-                nc.vector.tensor_copy(out=grouped[:, :v, :], in_=raw[a][:, :, t0 : t0 + v].rearrange("p j t -> p t j"))
-            if v < t1 - t0:
-                nc.scalar.copy(out=grouped[:, v:, :], in_=raw[a][:, :, t0 + v : t1].rearrange("p j t -> p t j"))
-            return grouped
+        def group(a, t0, t1):
+            return keep.tile([P, t1 - t0, 4], BF16, name=f"grouped{a}_{t0}", align_bytes=256)
+
+        def interleave(copy, grouped, a, base, t0, t1):
+            copy(
+                out=grouped[:, t0 - base : t1 - base, :].rearrange("p (c i) j -> p c j i", i=4),
+                in_=raw[a][:, :, t0:t1].rearrange("p j (c i) -> p c j i", i=4),
+            )
 
         def quant(a, t0, t1, grouped):
             row = 4 * (1 - a)
@@ -104,58 +124,62 @@ def tile_moe_rag_lin_none_kernel(
                 in_=grouped[:].rearrange("p t j -> p (t j)"),
             )
 
-        for (t0, t1), v in CHUNKS:
-            quant(0, t0, t1, quantise(0, t0, t1, v))
+        for t0, t1, v in CHUNKS0:
+            grouped = group(0, t0, t1)
+            interleave(nc.vector.tensor_copy, grouped, 0, t0, t0, t0 + v)
+            if t0 + v < t1:
+                interleave(nc.scalar.copy, grouped, 0, t0, t0 + v, t1)
+            quant(0, t0, t1, grouped)
 
         def gather(dst, src, s0, s1):
             nc.vector.tensor_copy(dst[:, s0:s1], src[:].indirect(offs_t[:, s0 // 16 : s1 // 16]))
 
-        g1 = [(t0, t1, quantise(1, t0, t1, 0)) for (t0, t1), v in CHUNKS1[:-1]]
         for s0, s1 in PIECES0[:2]:
             gather(slot_words[0], words[0], s0, s1)
-        for t0, t1, g in g1[:1]:
-            quant(1, t0, t1, g)
-        for s0, s1 in PIECES0[2:]:
-            gather(slot_words[0], words[0], s0, s1)
-        for t0, t1, g in g1[1:]:
-            quant(1, t0, t1, g)
-        for (t0, t1), v in CHUNKS1[-1:]:
-            quant(1, t0, t1, quantise(1, t0, t1, v))
-
-        def matmuls(bank, h, expert, col, count):
-            n0 = expert * N + h * P
-            s0 = STARTS[expert]
-            step = 512 if count == 512 else 128
-            for c in range(0, count, step):
-                s = slice(s0 + c, s0 + c + step)
-                nc.tensor.matmul_mx(
-                    out=bank[:, col + c : col + c + step],
-                    lhsT=w4[:, 2 * n0 : 2 * (n0 + P)].bitcast(E2M1X4),
-                    lhsT_scale=w_scales[:, n0 : n0 + P],
-                    rhs=slot_words[1][:, s].bitcast(E4M3X4),
-                    rhs_scale=slot_scales[:, s],
-                    start=True,
-                    stop=False,
-                )
-                nc.tensor.matmul_mx(
-                    out=bank[:, col + c : col + c + step],
-                    lhsT=w8[:, n0 : n0 + P].bitcast(E4M3X4),
-                    lhsT_scale=w_scales[4:P, n0 : n0 + P],
-                    rhs=slot_words[0][:, s].bitcast(E4M3X4),
-                    rhs_scale=slot_scales[4:P, s],
-                    start=False,
-                    stop=True,
-                )
-
-        for b, (byte_pieces, pieces, members, copies) in enumerate(GROUPS):
-            for s0, s1 in byte_pieces:
+        grouped = group(1, 0, 512)
+        interleave(nc.scalar.copy, grouped, 1, 0, 0, 256)
+        interleave(nc.scalar.copy, grouped, 1, 0, 256, 512)
+        quant(1, 0, 512, grouped)
+        gather(slot_words[0], words[0], *PIECES0[2])
+        grouped = group(1, 512, 768)
+        interleave(nc.vector.tensor_copy, grouped, 1, 512, 512, 608)
+        interleave(nc.scalar.copy, grouped, 1, 512, 608, 768)
+        quant(1, 512, 768, grouped)
+        gather(slot_words[0], words[0], *PIECES0[3])
+        for kind, s0, s1 in STEPS:
+            if kind == "bytes":
                 gather(slot_scales, scales, s0, s1)
-            for s0, s1 in pieces:
+            else:
                 gather(slot_words[1], words[1], s0, s1)
-            for h in range(2):
-                bank = psum.tile([P, 512], F32, name=f"bank{b}{h}")
+
+        def product(out_cols, e, h, s, fmt, start):
+            n0 = e * N + h * P
+            if fmt == "e4m3":
+                lhsT, row, a = w8[:, n0 : n0 + P].bitcast(E4M3X4), 4, 0
+            else:
+                lhsT, row, a = w4[:, 2 * n0 : 2 * (n0 + P)].bitcast(E2M1X4), 0, 1
+            nc.tensor.matmul_mx(
+                out=out_cols,
+                lhsT=lhsT,
+                lhsT_scale=w_scales[row:P, n0 : n0 + P],
+                rhs=slot_words[a][:, s].bitcast(E4M3X4),
+                rhs_scale=slot_scales[row:P, s],
+                start=start,
+                stop=not start,
+            )
+
+        for h in range(2):
+            banks = [psum.tile([P, 512], F32, name=f"bank{b}{h}") for b in range(4)]
+            for (members, copies), b in zip(BANKS, BANK_OF):
+                bank = banks[b]
                 for e, col in members:
-                    matmuls(bank, h, e, col, STARTS[e + 1] - STARTS[e])
+                    count = STARTS[e + 1] - STARTS[e]
+                    step = 512 if count == 512 else 128
+                    for c in range(0, count, step):
+                        cols = bank[:, col + c : col + c + step]
+                        s = slice(STARTS[e] + c, STARTS[e] + c + step)
+                        product(cols, e, h, s, "e2m1", True)
+                        product(cols, e, h, s, "e4m3", False)
                 for s0, col, n in copies:
                     nc.scalar.copy(out=y[h][:, s0 : s0 + n], in_=bank[:, col : col + n])
 

@@ -142,8 +142,8 @@ def tile_moe_rag_lin_none_kernel(
         quant(1, 0, 512, grouped)
         gather(slot_words[0], words[0], *PIECES0[2])
         grouped = group(1, 512, 768)
-        interleave(nc.vector.tensor_copy, grouped, 1, 512, 512, 608)
-        interleave(nc.scalar.copy, grouped, 1, 512, 608, 768)
+        interleave(nc.vector.tensor_copy, grouped, 1, 512, 512, 640)
+        interleave(nc.scalar.copy, grouped, 1, 512, 640, 768)
         quant(1, 512, 768, grouped)
         gather(slot_words[0], words[0], *PIECES0[3])
         for kind, s0, s1 in STEPS:
@@ -178,8 +178,8 @@ def tile_moe_rag_lin_none_kernel(
                     for c in range(0, count, step):
                         cols = bank[:, col + c : col + c + step]
                         s = slice(STARTS[e] + c, STARTS[e] + c + step)
-                        product(cols, e, h, s, "e2m1", True)
-                        product(cols, e, h, s, "e4m3", False)
+                        product(cols, e, h, s, "e4m3", True)
+                        product(cols, e, h, s, "e2m1", False)
                 for s0, col, n in copies:
                     nc.scalar.copy(out=y[h][:, s0 : s0 + n], in_=bank[:, col : col + n])
 

@@ -19,7 +19,7 @@ P = 128
 FLOPS = 2 * K * N * S
 
 STARTS = (0, 128, 256, 384, 768, 1280, 1536)
-CHUNKS0 = ((0, 256, 256), (256, 512, 176), (512, 768, 192))
+CHUNKS0 = ((0, 256, 256), (256, 512, 176), (512, 640, 0), (640, 768, 96))
 CHUNKS1 = ((0, 512, (0, 256)), (512, 768, (512,)))
 PIECES0 = ((0, 512), (512, 1024), (1024, 1408), (1408, 1536))
 STEPS = (
@@ -124,27 +124,33 @@ def tile_moe_rag_lin_none_kernel(
                 in_=grouped[:].rearrange("p t j -> p (t j)"),
             )
 
-        for t0, t1, v in CHUNKS0:
-            grouped = group(0, t0, t1)
-            interleave(nc.vector.tensor_copy, grouped, 0, t0, t0, t0 + v)
+        def interleave_shared(grouped, a, t0, t1, v):
+            if v > 0:
+                interleave(nc.vector.tensor_copy, grouped, a, t0, t0, t0 + v)
             if t0 + v < t1:
-                interleave(nc.scalar.copy, grouped, 0, t0, t0 + v, t1)
-            quant(0, t0, t1, grouped)
+                interleave(nc.scalar.copy, grouped, a, t0, t0 + v, t1)
+
+        groups0 = [group(0, t0, t1) for t0, t1, v in CHUNKS0]
+        for g, (t0, t1, v) in list(zip(groups0, CHUNKS0))[:2]:
+            interleave_shared(g, 0, t0, t1, v)
+            quant(0, t0, t1, g)
+        for g, (t0, t1, v) in list(zip(groups0, CHUNKS0))[2:]:
+            interleave_shared(g, 0, t0, t1, v)
+        for g, (t0, t1, v) in list(zip(groups0, CHUNKS0))[2:]:
+            quant(0, t0, t1, g)
 
         def gather(dst, src, s0, s1):
             nc.vector.tensor_copy(dst[:, s0:s1], src[:].indirect(offs_t[:, s0 // 16 : s1 // 16]))
 
-        for s0, s1 in PIECES0[:2]:
+        for s0, s1 in PIECES0[:3]:
             gather(slot_words[0], words[0], s0, s1)
-        grouped = group(1, 0, 512)
-        interleave(nc.scalar.copy, grouped, 1, 0, 0, 256)
-        interleave(nc.scalar.copy, grouped, 1, 0, 256, 512)
-        quant(1, 0, 512, grouped)
-        gather(slot_words[0], words[0], *PIECES0[2])
-        grouped = group(1, 512, 768)
-        interleave(nc.vector.tensor_copy, grouped, 1, 512, 512, 640)
-        interleave(nc.scalar.copy, grouped, 1, 512, 640, 768)
-        quant(1, 512, 768, grouped)
+        grouped_ab = group(1, 0, 512)
+        interleave_shared(grouped_ab[:, 0:256, :], 1, 0, 256, 0)
+        interleave_shared(grouped_ab[:, 256:512, :], 1, 256, 512, 0)
+        grouped_c = group(1, 512, 768)
+        interleave_shared(grouped_c, 1, 512, 768, 64)
+        quant(1, 0, 512, grouped_ab)
+        quant(1, 512, 768, grouped_c)
         gather(slot_words[0], words[0], *PIECES0[3])
         for kind, s0, s1 in STEPS:
             if kind == "bytes":
@@ -198,5 +204,5 @@ def tile_moe_rag_lin_none_kernel(
         total(0, 0, T)
         fetch(1, 1, 0, 512)
         fetch(1, 1, 512, T)
-        total(1, 0, 512)
-        total(1, 512, T)
+        for t0 in range(0, T, 256):
+            total(1, t0, t0 + 256)

from contextlib import ExitStack

import concourse.mybir as mybir

F32 = mybir.dt.float32
BF16 = mybir.dt.bfloat16
I32 = mybir.dt.int32
U32 = mybir.dt.uint32
U16 = mybir.dt.uint16
U8 = mybir.dt.uint8
E4M3X4 = mybir.dt.float8_e4m3fn_x4
E2M1X4 = mybir.dt.float4_e2m1fn_x4
MULT = mybir.AluOpType.mult
ADD = mybir.AluOpType.add

K, T, E, N = 1024, 768, 6, 256
S = 2 * T
P = 128
FLOPS = 2 * K * N * S

STARTS = (0, 128, 256, 384, 768, 1280, 1536)
CHUNKS0 = ((0, 256, 256), (256, 512, 176), (512, 640, 0), (640, 768, 96))
CHUNKS1 = ((0, 512, (0, 256)), (512, 768, (512,)))
PIECES0 = ((0, 512), (512, 1024), (1024, 1408), (1408, 1536))
STEPS = (
    ("bytes", 960, 1536),
    ("words", 1280, 1536),
    ("bytes", 384, 960),
    ("words", 768, 1280),
    ("words", 384, 768),
    ("bytes", 0, 256),
    ("words", 0, 256),
    ("bytes", 256, 384),
    ("words", 256, 384),
)
BANKS = (
    (((5, 0),), ((1280, 0, 256),)),
    (((4, 0),), ((768, 0, 512),)),
    (((3, 0),), ((384, 0, 384),)),
    (((0, 256), (1, 384)), ((0, 256, 256),)),
    (((2, 0),), ((256, 0, 128),)),
)
BANK_OF = (0, 1, 2, 0, 3)


def tile_moe_rag_lin_none_kernel(
    tc, xT, w8_words, w8_scales, w4_words, w4_scales, gate, offs, pos1, pos2, out
):
    nc = tc.nc
    with ExitStack() as ctx:
        keep = ctx.enter_context(tc.tile_pool(name="keep", bufs=1))
        psum = ctx.enter_context(tc.psum_pool(name="psum", bufs=1))

        offs_t = keep.tile([P, S // 16], U16, name="offs_t")
        pos_t = [keep.tile([P, T // 16], U16, name=f"pos_t{i}") for i in range(2)]
        raw = [keep.tile([P, 4, T], F32, name=f"raw{a}") for a in range(2)]
        words = [keep.tile([P, T], U32, name=f"words{a}", align_bytes=256) for a in range(2)]
        scales = keep.tile([P, T], U8, name="scales", align_bytes=256)
        slot_words = [keep.tile([P, S], U32, name=f"slot_words{a}", align_bytes=256) for a in range(2)]
        slot_scales = keep.tile([P, S], U8, name="slot_scales", align_bytes=256)
        w8 = keep.tile([P, E * N], U32, name="w8", align_bytes=256)
        w4 = keep.tile([P, E * 2 * N], U8, name="w4", align_bytes=256)
        w_scales_i = keep.tile([P, E * N // 4], I32, name="w_scales_i", align_bytes=256)
        w_scales = w_scales_i[:].bitcast(U8)
        gates = [[keep.tile([P, T], F32, name=f"gate{c}{h}") for h in range(2)] for c in range(2)]
        y = [keep.tile([P, S], F32, name=f"y{h}") for h in range(2)]
        prod = [[keep.tile([P, T], F32, name=f"prod{c}{h}") for h in range(2)] for c in range(2)]
        res = [keep.tile([P, T], F32, name=f"res{h}") for h in range(2)]

        nc.gpsimd.memset(scales[:], 0)
        nc.vector.memset(w_scales_i[:], 0)

        def load_x(a, t0, t1):
            nc.sync.dma_start(
                out=raw[a][:, :, t0:t1],
                in_=xT[512 * a : 512 * (a + 1), t0:t1].rearrange("(p j) t -> p j t", j=4),
            )

        for t0, t1, v in CHUNKS0:
            load_x(0, t0, t1)
        nc.sync.dma_start(offs_t[:], offs)
        for t0, t1, loads in CHUNKS1:
            for c0 in loads:
                load_x(1, c0, c0 + 256)
        def load_scales(src, row, q):
            nc.sync.dma_start(
                out=w_scales_i[32 * q + row : 32 * q + row + 4, :].rearrange("p (e n) -> p e n", e=E),
                in_=src[:, 0, 4 * q : 4 * q + 4, :].rearrange("e q n -> q e n").bitcast(I32),
            )

        scale_loads = [(src, row, q) for src, row in ((w4_scales, 0), (w8_scales, 4)) for q in range(4)]
        for src, row, q in scale_loads[:5]:
            load_scales(src, row, q)
        nc.sync.dma_start(
            out=w4[:].bitcast(I32).rearrange("p (e n) -> p e n", e=E),
            in_=w4_words.rearrange("e a p b -> p (e a) b").bitcast(I32),
        )
        nc.sync.dma_start(
            out=w8[:].bitcast(I32).rearrange("p (e n) -> p e n", e=E),
            in_=w8_words.rearrange("e a p n t -> p (e a) (n t)").bitcast(I32),
        )
        for src, row, q in scale_loads[5:]:
            load_scales(src, row, q)
        nc.sync.dma_start(pos_t[0][:], pos1)
        nc.sync.dma_start(pos_t[1][:], pos2)
        for h in range(2):
            for c in range(2):
                nc.sync.dma_start(gates[c][h][:], gate[c, P * h : P * (h + 1), :])

        def group(a, t0, t1):
            return keep.tile([P, t1 - t0, 4], BF16, name=f"grouped{a}_{t0}", align_bytes=256)

        def interleave(copy, grouped, a, base, t0, t1):
            copy(
                out=grouped[:, t0 - base : t1 - base, :].rearrange("p (c i) j -> p c j i", i=4),
                in_=raw[a][:, :, t0:t1].rearrange("p j (c i) -> p c j i", i=4),
            )

        def quant(a, t0, t1, grouped):
            row = 4 * (1 - a)
            nc.vector.quantize_mx(
                out=words[a][:, t0:t1].bitcast(E4M3X4),
                scales=scales[row:P, t0:t1],
                in_=grouped[:].rearrange("p t j -> p (t j)"),
            )

        def interleave_shared(grouped, a, t0, t1, v):
            if v > 0:
                interleave(nc.vector.tensor_copy, grouped, a, t0, t0, t0 + v)
            if t0 + v < t1:
                interleave(nc.scalar.copy, grouped, a, t0, t0 + v, t1)

        groups0 = [group(0, t0, t1) for t0, t1, v in CHUNKS0]
        for g, (t0, t1, v) in list(zip(groups0, CHUNKS0))[:2]:
            interleave_shared(g, 0, t0, t1, v)
            quant(0, t0, t1, g)
        for g, (t0, t1, v) in list(zip(groups0, CHUNKS0))[2:]:
            interleave_shared(g, 0, t0, t1, v)
        for g, (t0, t1, v) in list(zip(groups0, CHUNKS0))[2:]:
            quant(0, t0, t1, g)

        def gather(dst, src, s0, s1):
            nc.vector.tensor_copy(dst[:, s0:s1], src[:].indirect(offs_t[:, s0 // 16 : s1 // 16]))

        for s0, s1 in PIECES0[:3]:
            gather(slot_words[0], words[0], s0, s1)
        grouped_ab = group(1, 0, 512)
        interleave_shared(grouped_ab[:, 0:256, :], 1, 0, 256, 0)
        interleave_shared(grouped_ab[:, 256:512, :], 1, 256, 512, 0)
        grouped_c = group(1, 512, 768)
        interleave_shared(grouped_c, 1, 512, 768, 64)
        quant(1, 0, 512, grouped_ab)
        quant(1, 512, 768, grouped_c)
        gather(slot_words[0], words[0], *PIECES0[3])
        for kind, s0, s1 in STEPS:
            if kind == "bytes":
                gather(slot_scales, scales, s0, s1)
            else:
                gather(slot_words[1], words[1], s0, s1)

        def product(out_cols, e, h, s, fmt, start):
            n0 = e * N + h * P
            if fmt == "e4m3":
                lhsT, row, a = w8[:, n0 : n0 + P].bitcast(E4M3X4), 4, 0
            else:
                lhsT, row, a = w4[:, 2 * n0 : 2 * (n0 + P)].bitcast(E2M1X4), 0, 1
            nc.tensor.matmul_mx(
                out=out_cols,
                lhsT=lhsT,
                lhsT_scale=w_scales[row:P, n0 : n0 + P],
                rhs=slot_words[a][:, s].bitcast(E4M3X4),
                rhs_scale=slot_scales[row:P, s],
                start=start,
                stop=not start,
            )

        for h in range(2):
            banks = [psum.tile([P, 512], F32, name=f"bank{b}{h}") for b in range(4)]
            for (members, copies), b in zip(BANKS, BANK_OF):
                bank = banks[b]
                for e, col in members:
                    count = STARTS[e + 1] - STARTS[e]
                    step = 512 if count == 512 else 128
                    for c in range(0, count, step):
                        cols = bank[:, col + c : col + c + step]
                        s = slice(STARTS[e] + c, STARTS[e] + c + step)
                        product(cols, e, h, s, "e4m3", True)
                        product(cols, e, h, s, "e2m1", False)
                for s0, col, n in copies:
                    nc.scalar.copy(out=y[h][:, s0 : s0 + n], in_=bank[:, col : col + n])

        def fetch(c, h, t0, t1):
            nc.vector.tensor_tensor(
                prod[c][h][:, t0:t1], y[h][:].indirect(pos_t[c][:, t0 // 16 : t1 // 16]), gates[c][h][:, t0:t1], MULT
            )

        def total(h, t0, t1):
            nc.vector.tensor_tensor(res[h][:, t0:t1], prod[0][h][:, t0:t1], prod[1][h][:, t0:t1], ADD)
            nc.sync.dma_start(out[P * h : P * (h + 1), t0:t1], res[h][:, t0:t1])

        fetch(0, 0, 0, T)
        fetch(1, 0, 0, T)
        fetch(0, 1, 0, T)
        total(0, 0, T)
        fetch(1, 1, 0, 512)
        fetch(1, 1, 512, T)
        for t0 in range(0, T, 256):
            total(1, t0, t0 + 256)
